import numpy as np
CORES = [24,27,29,56,59,61,88,91,93,120,123,125]
N = 12
KT, F = 1, 128
def setup_inputs(rng):
    return {"a": rng.standard_normal((N, 128, KT * 128), dtype=np.float32), "w": rng.standard_normal((N, 128, KT * F), dtype=np.float32)}
def reference(a, w):
    A, W = a.astype(np.float64), w.astype(np.float64)
    y = np.zeros((N, 128, N * F))
    for r in range(N):
        for j in range(N):
            for t in range(KT):
                y[r][:, F * j:F * j + F] += A[j][:, 128 * t:128 * t + 128].T @ W[r][:, F * t:F * t + F]
    return {"y": y.astype(np.float32 if a.dtype != np.float64 else np.float64)}

@@ -1,0 +1,174 @@
+from concourse.bass import DstId, RemoteDMATransfer
+
+B = 128
+NR = 12
+
+SCRATCH = {
+    "wbuf": ("sbuf", [128, B], "float32"),
+    "ag": ("sbuf", [128, NR * B], "float32"),
+    "out": ("sbuf", [128, NR * B], "float32"),
+    "ps0": ("psum", [128, 512], "float32"),
+    "ps1": ("psum", [128, 512], "float32"),
+    "ps2": ("psum", [128, 512], "float32"),
+    "ps3": ("psum", [128, 512], "float32"),
+    "ps4": ("psum", [128, 512], "float32"),
+    "ps5": ("psum", [128, 512], "float32"),
+}
+SEMAPHORES = ["la", "lw", "sent", "pe", "d1", "d2", "d3", "f1", "f2", "f3",
+              "mm0", "mm1", "mm2", "mm3", "mm4", "mm5", "cp0", "cp1", "cp2", "cp3", "sta", "stb"]
+
+
+def _bits(m):
+    return [b for b in range(m.bit_length()) if (m >> b) & 1]
+
+
+def _count(m):
+    return len(_bits(m))
+
+
+def _split(m, k):
+    bs = _bits(m)
+    n = len(bs) // k
+    return [sum(1 << b for b in bs[i * n:(i + 1) * n]) for i in range(k)]
+
+
+def _layout(T, topo):
+    chips, members = [], {}
+    for c in T.cores:
+        ch = topo.chip(c)
+        if ch not in members:
+            members[ch] = []
+            chips.append(ch)
+        members[ch].append(c)
+    return chips, members
+
+
+def _stage_sends(cores, last, topo):
+    plan = {c: [c] for c in cores}
+    by = {}
+    for c in cores:
+        by.setdefault(topo.die(c), []).append(c)
+    dies = sorted(by, key=lambda d: -len(by[d]))
+    if last and len(dies) == 2 and len(by[dies[0]]) > len(by[dies[1]]):
+        owner, sender = by[dies[0]][-1], by[dies[1]][0]
+        plan[owner] = []
+        plan[sender] = [sender, owner]
+    return plan
+
+
+def rank_program(g, core, T, topo):
+    rank = T.rank_of(core)
+    if rank is None:
+        return
+    S = T.sem
+    chips, members = _layout(T, topo)
+    nch = len(chips)
+    ci = chips.index(topo.chip(core))
+    mine = members[chips[ci]]
+    p = mine.index(core)
+    peers = [c for c in mine if c != core]
+    stages = list(range(1, nch))
+
+    def cols(c, n=1):
+        j = T.rank_of(c)
+        return slice(j * B, (j + n) * B)
+
+    def blk(c):
+        return T.ag[:, cols(c)]
+
+    def did(c):
+        rid, pid, _ = topo.addr(c)
+        return DstId(rid=rid, pnc=pid)
+
+    def src_chip(s):
+        return members[chips[(ci - s) % nch]]
+
+    def direct_engines(s):
+        src = src_chip(s)
+        for sender, owners in _stage_sends(src, s == stages[-1], topo).items():
+            if src[p] in owners:
+                return _count(topo.mask(sender, core)) // len(owners)
+
+    on = topo.mask(core, peers[0])
+    off = topo.mask(core, members[chips[(ci + 1) % nch]][0])
+    on_only = on & ~off
+    n_pe = len(peers) * _count(on_only)
+    n_fw = len(peers) * _count(on)
+
+    g.sync.dma_start(blk(core), T.a[:]).then_inc(S.la, 16)
+    g.scalar.dma_start(T.wbuf[:], T.w[:]).then_inc(S.lw, 16)
+
+    sent = 0
+    g.wait_ge(S.la, 16)
+    for s in stages:
+        dst = members[chips[(ci + s) % nch]]
+        owners = _stage_sends(mine, s == stages[-1], topo)[core]
+        trs = []
+        if s == 1:
+            trs.append(RemoteDMATransfer(dst_ids=[did(c) for c in peers], dma_engine_mask=on_only, remote_sem=S.pe,
+                                         srcs=[blk(core)], dsts=[blk(core) for _ in peers]))
+            sent += _count(on_only)
+        if any(o != core for o in owners):
+            g.wait_ge(S.pe, n_pe)
+        if owners:
+            for o, m in zip(owners, _split(off, len(owners))):
+                trs.append(RemoteDMATransfer(dst_ids=[did(dst[mine.index(o)])], dma_engine_mask=m,
+                                             remote_sem=S["d%d" % s], srcs=[blk(o)], dsts=[blk(o)]))
+                sent += _count(m)
+        if trs:
+            g.remote_dma_fused(trs, local_sem=S.sent)
+    for s in stages:
+        o = src_chip(s)[p]
+        g.wait_ge(S["d%d" % s], direct_engines(s))
+        g.remote_dma_fused([RemoteDMATransfer(dst_ids=[did(c) for c in peers], dma_engine_mask=on,
+                                              remote_sem=S["f%d" % s], srcs=[blk(o)], dsts=[blk(o) for _ in peers])],
+                           local_sem=S.sent)
+        sent += _count(on)
+    g.wait_ge(S.sent, sent)
+
+    te = g.tensor
+
+    def mm(ps, col, c, sem):
+        te.matmul(ps[:, col:col + B], blk(c), T.wbuf[:], True, True).then_inc(sem, 1)
+
+    te.wait_ge(S.la, 16)
+    te.wait_ge(S.lw, 16)
+    mm(T.ps0, p * B, core, S.mm0)
+    te.wait_ge(S.pe, n_pe)
+    for c in peers:
+        mm(T.ps0, mine.index(c) * B, c, S.mm0)
+    last_order = []
+    for s in stages:
+        src = src_chip(s)
+        order = [src[p]] + [c for c in src if c != src[p]]
+        for k, c in enumerate(order):
+            if k == 0:
+                te.wait_ge(S["d%d" % s], direct_engines(s))
+            if k == 1:
+                te.wait_ge(S["f%d" % s], n_fw)
+            if s != stages[-1]:
+                mm(T["ps%d" % s], src.index(c) * B, c, S["mm%d" % s])
+            else:
+                mm(T["ps%d" % (s + k)], 0, c, S["mm%d" % (s + k)])
+                last_order.append(c)
+
+    ve = g.vector
+    for grp in range(nch - 1):
+        src = src_chip(grp)
+        ve.wait_ge(S["mm%d" % grp], len(src))
+        ve.tensor_copy(T.out[:, cols(src[0], len(src))], T["ps%d" % grp][:, 0:len(src) * B]).then_inc(S["cp%d" % grp], 1)
+    for k, c in enumerate(last_order):
+        ve.wait_ge(S["mm%d" % (nch - 1 + k)], 1)
+        ve.tensor_copy(T.out[:, cols(c)], T["ps%d" % (nch - 1 + k)][:, 0:B]).then_inc(S["cp%d" % (nch - 1)], 1)
+
+    queues = [(g.sync, S.sta), (g.scalar, S.stb)]
+    issued = [0, 0]
+    for grp in range(nch):
+        src = src_chip(grp)
+        q, sem = queues[grp % 2]
+        q.wait_ge(S["cp%d" % grp], 1 if grp < nch - 1 else len(src))
+        cs = cols(src[0], len(src))
+        q.dma_start(T.y[:, cs], T.out[:, cs]).then_inc(sem, 16)
+        issued[grp % 2] += 16
+    for (q, sem), n in zip(queues, issued):
+        q.wait_ge(sem, n)

@@ -13,9 +13,12 @@ SCRATCH = {
     "ps3": ("psum", [128, 512], "float32"),
     "ps4": ("psum", [128, 512], "float32"),
     "ps5": ("psum", [128, 512], "float32"),
+    "ps6": ("psum", [128, 512], "float32"),
+    "ps7": ("psum", [128, 512], "float32"),
 }
-SEMAPHORES = ["la", "lw", "sent", "pe", "d1", "d2", "d3", "f1", "f2", "f3",
-              "mm0", "mm1", "mm2", "mm3", "mm4", "mm5", "cp0", "cp1", "cp2", "cp3", "sta", "stb"]
+SEMAPHORES = (["la", "lw", "sent", "pe", "d1", "d2", "d3"]
+              + ["f%d%d" % (s, q) for s in (1, 2, 3) for q in (0, 1, 2)]
+              + ["mm%d" % k for k in range(8)] + ["cp0", "cp1", "cp2", "cp3", "sta", "stb"])
 
 
 def _bits(m):
@@ -43,31 +46,36 @@ def _layout(T, topo):
     return chips, members
 
 
-def _stage_sends(cores, last, topo):
-    plan = {c: [c] for c in cores}
+def _chip_cores(ch, topo):
+    return [c for c in range(topo.CHIPS * topo.CORES_PER_CHIP) if topo.chip(c) == ch]
+
+
+def _mate_cores(ch, topo):
+    return [c for m in range(topo.CHIPS) if topo.mates(m, ch) for c in _chip_cores(m, topo)]
+
+
+def _roles(cores, topo):
     by = {}
     for c in cores:
         by.setdefault(topo.die(c), []).append(c)
     dies = sorted(by, key=lambda d: -len(by[d]))
-    if last and len(dies) == 2 and len(by[dies[0]]) > len(by[dies[1]]):
-        owner, sender = by[dies[0]][-1], by[dies[1]][0]
-        plan[owner] = []
-        plan[sender] = [sender, owner]
-    return plan
+    over = _mate_cores(topo.chip(cores[0]), topo)[0]
+    x = [c for c in by[dies[0]] if topo.may_write(c, over)][-1]
+    return x, by[dies[1]][0]
+
+
+def _relay(x_dst, T, topo):
+    ok = [c for c in _mate_cores(topo.chip(x_dst), topo) if T.rank_of(c) is None and topo.may_write(c, x_dst)]
+    same = [c for c in ok if topo.die(c) == topo.die(x_dst)]
+    return (same or ok)[0]
 
 
 def rank_program(g, core, T, topo):
-    rank = T.rank_of(core)
-    if rank is None:
-        return
     S = T.sem
     chips, members = _layout(T, topo)
     nch = len(chips)
-    ci = chips.index(topo.chip(core))
-    mine = members[chips[ci]]
-    p = mine.index(core)
-    peers = [c for c in mine if c != core]
-    stages = list(range(1, nch))
+    roles = [_roles(members[ch], topo) for ch in chips]
+    relays = [_relay(roles[i][0], T, topo) for i in range(nch)]
 
     def cols(c, n=1):
         j = T.rank_of(c)
@@ -80,53 +88,83 @@ def rank_program(g, core, T, topo):
         rid, pid, _ = topo.addr(c)
         return DstId(rid=rid, pnc=pid)
 
+    def one(dsts, mask, sem, c):
+        return RemoteDMATransfer(dst_ids=[did(d) for d in dsts], dma_engine_mask=mask, remote_sem=sem,
+                                 srcs=[blk(c)], dsts=[blk(c) for _ in dsts])
+
+    rank = T.rank_of(core)
+    if rank is None:
+        if core in relays:
+            i = relays.index(core)
+            x_src, x_dst = roles[(i - 2) % nch][0], roles[i][0]
+            m = topo.mask(core, x_dst)
+            g.wait_ge(S.pe, _count(topo.mask(x_src, core)) // 2)
+            g.remote_dma_fused([one([x_dst], m, S.d2, x_src)], local_sem=S.sent)
+            g.wait_ge(S.sent, _count(m))
+        return
+
+    ci = chips.index(topo.chip(core))
+    mine = members[chips[ci]]
+    p = mine.index(core)
+    peers = [c for c in mine if c != core]
+    X, P = roles[ci]
+    xp, pp = mine.index(X), mine.index(P)
+
     def src_chip(s):
         return members[chips[(ci - s) % nch]]
 
-    def direct_engines(s):
-        src = src_chip(s)
-        for sender, owners in _stage_sends(src, s == stages[-1], topo).items():
-            if src[p] in owners:
-                return _count(topo.mask(sender, core)) // len(owners)
+    def dst_chip(s):
+        return members[chips[(ci + s) % nch]]
 
     on = topo.mask(core, peers[0])
-    off = topo.mask(core, members[chips[(ci + 1) % nch]][0])
+    off = topo.mask(core, dst_chip(1)[0])
     on_only = on & ~off
+    halves = _split(off, 2)
     n_pe = len(peers) * _count(on_only)
-    n_fw = len(peers) * _count(on)
+    n_off, n_half, n_on = _count(off), _count(halves[0]), _count(on)
+    n_d = {1: n_half if p == xp else n_off, 2: n_off, 3: n_half if p in (xp, pp) else n_off}
 
     g.sync.dma_start(blk(core), T.a[:]).then_inc(S.la, 16)
     g.scalar.dma_start(T.wbuf[:], T.w[:]).then_inc(S.lw, 16)
 
     sent = 0
     g.wait_ge(S.la, 16)
-    for s in stages:
-        dst = members[chips[(ci + s) % nch]]
-        owners = _stage_sends(mine, s == stages[-1], topo)[core]
-        trs = []
-        if s == 1:
-            trs.append(RemoteDMATransfer(dst_ids=[did(c) for c in peers], dma_engine_mask=on_only, remote_sem=S.pe,
-                                         srcs=[blk(core)], dsts=[blk(core) for _ in peers]))
-            sent += _count(on_only)
-        if any(o != core for o in owners):
+    first = one(peers, on_only, S.pe, core)
+    if core == X:
+        g.remote_dma_fused([first, one([dst_chip(1)[p]], halves[0], S.d1, core),
+                            one([relays[(ci + 2) % nch]], halves[1], S.pe, core)], local_sem=S.sent)
+        sent += _count(on_only) + 2 * n_half
+    else:
+        g.remote_dma_fused([first, one([dst_chip(1)[p]], off, S.d1, core)], local_sem=S.sent)
+        g.remote_dma_fused([one([dst_chip(2)[p]], off, S.d2, core)], local_sem=S.sent)
+        sent += _count(on_only) + 2 * n_off
+        if core == P:
             g.wait_ge(S.pe, n_pe)
-        if owners:
-            for o, m in zip(owners, _split(off, len(owners))):
-                trs.append(RemoteDMATransfer(dst_ids=[did(dst[mine.index(o)])], dma_engine_mask=m,
-                                             remote_sem=S["d%d" % s], srcs=[blk(o)], dsts=[blk(o)]))
-                sent += _count(m)
-        if trs:
-            g.remote_dma_fused(trs, local_sem=S.sent)
-    for s in stages:
-        o = src_chip(s)[p]
-        g.wait_ge(S["d%d" % s], direct_engines(s))
-        g.remote_dma_fused([RemoteDMATransfer(dst_ids=[did(c) for c in peers], dma_engine_mask=on,
-                                              remote_sem=S["f%d" % s], srcs=[blk(o)], dsts=[blk(o) for _ in peers])],
-                           local_sem=S.sent)
-        sent += _count(on)
+            g.remote_dma_fused([one([dst_chip(3)[p]], halves[0], S.d3, core),
+                                one([dst_chip(3)[xp]], halves[1], S.d3, X)], local_sem=S.sent)
+        else:
+            g.remote_dma_fused([one([dst_chip(3)[p]], off, S.d3, core)], local_sem=S.sent)
+        sent += n_off
+    for s in (1, 2, 3):
+        g.wait_ge(S["d%d" % s], n_d[s])
+        g.remote_dma_fused([one(peers, on, S["f%d%d" % (s, p)], src_chip(s)[p])], local_sem=S.sent)
+        sent += n_on
     g.wait_ge(S.sent, sent)
 
+    others = [q for q in range(len(mine)) if q != p]
+    if p == xp:
+        order = [(2, p), (3, p)] + [(2, q) for q in others] + [(3, q) for q in others]
+    else:
+        o = [q for q in others if q != xp][0]
+        order = [(2, p), (2, o), (3, p), (2, xp), (3, o), (3, xp)]
+
     te = g.tensor
+
+    def arrived(queue, s, q):
+        if q == p:
+            queue.wait_ge(S["d%d" % s], n_d[s])
+        else:
+            queue.wait_ge(S["f%d%d" % (s, q)], n_on)
 
     def mm(ps, col, c, sem):
         te.matmul(ps[:, col:col + B], blk(c), T.wbuf[:], True, True).then_inc(sem, 1)
@@ -137,36 +175,28 @@ def rank_program(g, core, T, topo):
     te.wait_ge(S.pe, n_pe)
     for c in peers:
         mm(T.ps0, mine.index(c) * B, c, S.mm0)
-    last_order = []
-    for s in stages:
-        src = src_chip(s)
-        order = [src[p]] + [c for c in src if c != src[p]]
-        for k, c in enumerate(order):
-            if k == 0:
-                te.wait_ge(S["d%d" % s], direct_engines(s))
-            if k == 1:
-                te.wait_ge(S["f%d" % s], n_fw)
-            if s != stages[-1]:
-                mm(T["ps%d" % s], src.index(c) * B, c, S["mm%d" % s])
-            else:
-                mm(T["ps%d" % (s + k)], 0, c, S["mm%d" % (s + k)])
-                last_order.append(c)
+    for q in [p] + others:
+        arrived(te, 1, q)
+        mm(T.ps1, q * B, src_chip(1)[q], S.mm1)
+    for k, (s, q) in enumerate(order):
+        arrived(te, s, q)
+        mm(T["ps%d" % (2 + k)], 0, src_chip(s)[q], S["mm%d" % (2 + k)])
 
     ve = g.vector
-    for grp in range(nch - 1):
+    for grp in (0, 1):
         src = src_chip(grp)
         ve.wait_ge(S["mm%d" % grp], len(src))
         ve.tensor_copy(T.out[:, cols(src[0], len(src))], T["ps%d" % grp][:, 0:len(src) * B]).then_inc(S["cp%d" % grp], 1)
-    for k, c in enumerate(last_order):
-        ve.wait_ge(S["mm%d" % (nch - 1 + k)], 1)
-        ve.tensor_copy(T.out[:, cols(c)], T["ps%d" % (nch - 1 + k)][:, 0:B]).then_inc(S["cp%d" % (nch - 1)], 1)
+    for k, (s, q) in enumerate(order):
+        ve.wait_ge(S["mm%d" % (2 + k)], 1)
+        ve.tensor_copy(T.out[:, cols(src_chip(s)[q])], T["ps%d" % (2 + k)][:, 0:B]).then_inc(S["cp%d" % s], 1)
 
     queues = [(g.sync, S.sta), (g.scalar, S.stb)]
     issued = [0, 0]
     for grp in range(nch):
         src = src_chip(grp)
         q, sem = queues[grp % 2]
-        q.wait_ge(S["cp%d" % grp], 1 if grp < nch - 1 else len(src))
+        q.wait_ge(S["cp%d" % grp], 1 if grp < 2 else len(src))
         cs = cols(src[0], len(src))
         q.dma_start(T.y[:, cs], T.out[:, cs]).then_inc(sem, 16)
         issued[grp % 2] += 16

@@ -18,7 +18,7 @@ SCRATCH = {
 }
 SEMAPHORES = (["la", "lw", "sent", "pe", "d1", "d2", "d3"]
               + ["f%d%d" % (s, q) for s in (1, 2, 3) for q in (0, 1, 2)]
-              + ["mm%d" % k for k in range(8)] + ["cp0", "cp1", "cp2", "cp3", "sta", "stb"])
+              + ["mm%d" % k for k in range(8)] + ["cp0", "cp1", "cp2", "cp30", "cp31", "cp32", "sta", "stb"])
 
 
 def _bits(m):
@@ -98,7 +98,7 @@ def rank_program(g, core, T, topo):
             i = relays.index(core)
             x_src, x_dst = roles[(i - 2) % nch][0], roles[i][0]
             m = topo.mask(core, x_dst)
-            g.wait_ge(S.pe, _count(topo.mask(x_src, core)) // 2)
+            g.wait_ge(S.pe, _count(topo.mask(x_src, core)))
             g.remote_dma_fused([one([x_dst], m, S.d2, x_src)], local_sem=S.sent)
             g.wait_ge(S.sent, _count(m))
         return
@@ -122,18 +122,18 @@ def rank_program(g, core, T, topo):
     halves = _split(off, 2)
     n_pe = len(peers) * _count(on_only)
     n_off, n_half, n_on = _count(off), _count(halves[0]), _count(on)
-    n_d = {1: n_half if p == xp else n_off, 2: n_off, 3: n_half if p in (xp, pp) else n_off}
+    n_d = {1: n_off, 2: n_off, 3: n_half if p in (xp, pp) else n_off}
 
     g.sync.dma_start(blk(core), T.a[:]).then_inc(S.la, 16)
-    g.scalar.dma_start(T.wbuf[:], T.w[:]).then_inc(S.lw, 16)
+    g.sync.dma_start(T.wbuf[:], T.w[:]).then_inc(S.lw, 16)
 
     sent = 0
     g.wait_ge(S.la, 16)
     first = one(peers, on_only, S.pe, core)
     if core == X:
-        g.remote_dma_fused([first, one([dst_chip(1)[p]], halves[0], S.d1, core),
-                            one([relays[(ci + 2) % nch]], halves[1], S.pe, core)], local_sem=S.sent)
-        sent += _count(on_only) + 2 * n_half
+        g.remote_dma_fused([first, one([relays[(ci + 2) % nch]], off, S.pe, core)], local_sem=S.sent)
+        g.remote_dma_fused([one([dst_chip(1)[p]], off, S.d1, core)], local_sem=S.sent)
+        sent += _count(on_only) + 2 * n_off
     else:
         g.remote_dma_fused([first, one([dst_chip(1)[p]], off, S.d1, core)], local_sem=S.sent)
         g.remote_dma_fused([one([dst_chip(2)[p]], off, S.d2, core)], local_sem=S.sent)
@@ -189,16 +189,25 @@ def rank_program(g, core, T, topo):
         ve.tensor_copy(T.out[:, cols(src[0], len(src))], T["ps%d" % grp][:, 0:len(src) * B]).then_inc(S["cp%d" % grp], 1)
     for k, (s, q) in enumerate(order):
         ve.wait_ge(S["mm%d" % (2 + k)], 1)
-        ve.tensor_copy(T.out[:, cols(src_chip(s)[q])], T["ps%d" % (2 + k)][:, 0:B]).then_inc(S["cp%d" % s], 1)
+        ve.tensor_copy(T.out[:, cols(src_chip(s)[q])], T["ps%d" % (2 + k)][:, 0:B]).then_inc(
+            S.cp2 if s == 2 else S["cp3%d" % q], 1)
 
-    queues = [(g.sync, S.sta), (g.scalar, S.stb)]
-    issued = [0, 0]
-    for grp in range(nch):
-        src = src_chip(grp)
-        q, sem = queues[grp % 2]
-        q.wait_ge(S["cp%d" % grp], 1 if grp < 2 else len(src))
-        cs = cols(src[0], len(src))
-        q.dma_start(T.y[:, cs], T.out[:, cs]).then_inc(sem, 16)
-        issued[grp % 2] += 16
-    for (q, sem), n in zip(queues, issued):
-        q.wait_ge(sem, n)
+    last = [q for (s, q) in order if s == 3]
+    issued = {"sta": 0, "stb": 0}
+
+    def store(queue, name, sem, need, cs):
+        queue.wait_ge(sem, need)
+        queue.dma_start(T.y[:, cs], T.out[:, cs]).then_inc(S[name], 16)
+        issued[name] += 16
+
+    def group(s):
+        return cols(src_chip(s)[0], len(mine))
+
+    store(g.sync, "sta", S.cp0, 1, group(0))
+    store(g.scalar, "stb", S.cp1, 1, group(1))
+    store(g.scalar, "stb", S["cp3%d" % last[0]], 1, cols(src_chip(3)[last[0]]))
+    store(g.sync, "sta", S.cp2, len(mine), group(2))
+    store(g.scalar, "stb", S["cp3%d" % last[1]], 1, cols(src_chip(3)[last[1]]))
+    store(g.sync, "sta", S["cp3%d" % last[2]], 1, cols(src_chip(3)[last[2]]))
+    g.sync.wait_ge(S.sta, issued["sta"])
+    g.scalar.wait_ge(S.stb, issued["stb"])

@@ -125,7 +125,7 @@ def rank_program(g, core, T, topo):
     n_d = {1: n_off, 2: n_off, 3: n_half if p in (xp, pp) else n_off}
 
     g.sync.dma_start(blk(core), T.a[:]).then_inc(S.la, 16)
-    g.sync.dma_start(T.wbuf[:], T.w[:]).then_inc(S.lw, 16)
+    g.scalar.dma_start(T.wbuf[:], T.w[:]).then_inc(S.lw, 16)
 
     sent = 0
     g.wait_ge(S.la, 16)
@@ -153,18 +153,16 @@ def rank_program(g, core, T, topo):
 
     others = [q for q in range(len(mine)) if q != p]
     if p == xp:
-        order = [(2, p), (3, p)] + [(2, q) for q in others] + [(3, q) for q in others]
+        seq = [(1, p), (2, p), (3, p)] + [(s, q) for s in (1, 2, 3) for q in others]
     else:
         o = [q for q in others if q != xp][0]
-        order = [(2, p), (2, o), (3, p), (2, xp), (3, o), (3, xp)]
+        seq = [(1, p), (2, p), (1, o), (3, p), (1, xp), (2, o), (2, xp), (3, o), (3, xp)]
+    bank = {}
+    for sq in seq:
+        if sq[0] != 1:
+            bank[sq] = 2 + len(bank)
 
     te = g.tensor
-
-    def arrived(queue, s, q):
-        if q == p:
-            queue.wait_ge(S["d%d" % s], n_d[s])
-        else:
-            queue.wait_ge(S["f%d%d" % (s, q)], n_on)
 
     def mm(ps, col, c, sem):
         te.matmul(ps[:, col:col + B], blk(c), T.wbuf[:], True, True).then_inc(sem, 1)
@@ -175,24 +173,38 @@ def rank_program(g, core, T, topo):
     te.wait_ge(S.pe, n_pe)
     for c in peers:
         mm(T.ps0, mine.index(c) * B, c, S.mm0)
-    for q in [p] + others:
-        arrived(te, 1, q)
-        mm(T.ps1, q * B, src_chip(1)[q], S.mm1)
-    for k, (s, q) in enumerate(order):
-        arrived(te, s, q)
-        mm(T["ps%d" % (2 + k)], 0, src_chip(s)[q], S["mm%d" % (2 + k)])
+    for (s, q) in seq:
+        if q == p:
+            te.wait_ge(S["d%d" % s], n_d[s])
+        else:
+            te.wait_ge(S["f%d%d" % (s, q)], n_on)
+        if s == 1:
+            mm(T.ps1, q * B, src_chip(1)[q], S.mm1)
+        else:
+            mm(T["ps%d" % bank[(s, q)]], 0, src_chip(s)[q], S["mm%d" % bank[(s, q)]])
 
     ve = g.vector
-    for grp in (0, 1):
-        src = src_chip(grp)
-        ve.wait_ge(S["mm%d" % grp], len(src))
-        ve.tensor_copy(T.out[:, cols(src[0], len(src))], T["ps%d" % grp][:, 0:len(src) * B]).then_inc(S["cp%d" % grp], 1)
-    for k, (s, q) in enumerate(order):
-        ve.wait_ge(S["mm%d" % (2 + k)], 1)
-        ve.tensor_copy(T.out[:, cols(src_chip(s)[q])], T["ps%d" % (2 + k)][:, 0:B]).then_inc(
-            S.cp2 if s == 2 else S["cp3%d" % q], 1)
+    ng = len(mine)
 
-    last = [q for (s, q) in order if s == 3]
+    def group(s):
+        return cols(src_chip(s)[0], ng)
+
+    ve.wait_ge(S.mm0, ng)
+    ve.tensor_copy(T.out[:, group(0)], T.ps0[:, 0:ng * B]).then_inc(S.cp0, 1)
+    seen = 0
+    for (s, q) in seq:
+        if s == 1:
+            seen += 1
+            if seen == ng:
+                ve.wait_ge(S.mm1, ng)
+                ve.tensor_copy(T.out[:, group(1)], T.ps1[:, 0:ng * B]).then_inc(S.cp1, 1)
+        else:
+            k = bank[(s, q)]
+            ve.wait_ge(S["mm%d" % k], 1)
+            ve.tensor_copy(T.out[:, cols(src_chip(s)[q])], T["ps%d" % k][:, 0:B]).then_inc(
+                S.cp2 if s == 2 else S["cp3%d" % q], 1)
+
+    last = [q for (s, q) in seq if s == 3]
     issued = {"sta": 0, "stb": 0}
 
     def store(queue, name, sem, need, cs):
@@ -200,13 +212,10 @@ def rank_program(g, core, T, topo):
         queue.dma_start(T.y[:, cs], T.out[:, cs]).then_inc(S[name], 16)
         issued[name] += 16
 
-    def group(s):
-        return cols(src_chip(s)[0], len(mine))
-
     store(g.sync, "sta", S.cp0, 1, group(0))
-    store(g.scalar, "stb", S.cp1, 1, group(1))
     store(g.scalar, "stb", S["cp3%d" % last[0]], 1, cols(src_chip(3)[last[0]]))
-    store(g.sync, "sta", S.cp2, len(mine), group(2))
+    store(g.scalar, "stb", S.cp1, 1, group(1))
+    store(g.sync, "sta", S.cp2, ng, group(2))
     store(g.scalar, "stb", S["cp3%d" % last[1]], 1, cols(src_chip(3)[last[1]]))
     store(g.sync, "sta", S["cp3%d" % last[2]], 1, cols(src_chip(3)[last[2]]))
     g.sync.wait_ge(S.sta, issued["sta"])

from concourse.bass import DstId, RemoteDMATransfer

B = 128
NR = 12

SCRATCH = {
    "wbuf": ("sbuf", [128, B], "float32"),
    "ag": ("sbuf", [128, NR * B], "float32"),
    "out": ("sbuf", [128, NR * B], "float32"),
    "ps0": ("psum", [128, 512], "float32"),
    "ps1": ("psum", [128, 512], "float32"),
    "ps2": ("psum", [128, 512], "float32"),
    "ps3": ("psum", [128, 512], "float32"),
    "ps4": ("psum", [128, 512], "float32"),
    "ps5": ("psum", [128, 512], "float32"),
    "ps6": ("psum", [128, 512], "float32"),
    "ps7": ("psum", [128, 512], "float32"),
}
SEMAPHORES = (["la", "lw", "sent", "pe", "d1", "d2", "d3"]
              + ["f%d%d" % (s, q) for s in (1, 2, 3) for q in (0, 1, 2)]
              + ["mm%d" % k for k in range(8)] + ["cp0", "cp1", "cp2", "cp30", "cp31", "cp32", "sta", "stb"])


def _bits(m):
    return [b for b in range(m.bit_length()) if (m >> b) & 1]


def _count(m):
    return len(_bits(m))


def _split(m, k):
    bs = _bits(m)
    n = len(bs) // k
    return [sum(1 << b for b in bs[i * n:(i + 1) * n]) for i in range(k)]


def _layout(T, topo):
    chips, members = [], {}
    for c in T.cores:
        ch = topo.chip(c)
        if ch not in members:
            members[ch] = []
            chips.append(ch)
        members[ch].append(c)
    return chips, members


def _chip_cores(ch, topo):
    return [c for c in range(topo.CHIPS * topo.CORES_PER_CHIP) if topo.chip(c) == ch]


def _mate_cores(ch, topo):
    return [c for m in range(topo.CHIPS) if topo.mates(m, ch) for c in _chip_cores(m, topo)]


def _roles(cores, topo):
    by = {}
    for c in cores:
        by.setdefault(topo.die(c), []).append(c)
    dies = sorted(by, key=lambda d: -len(by[d]))
    over = _mate_cores(topo.chip(cores[0]), topo)[0]
    x = [c for c in by[dies[0]] if topo.may_write(c, over)][-1]
    return x, by[dies[1]][0]


def _relay(x_dst, T, topo):
    ok = [c for c in _mate_cores(topo.chip(x_dst), topo) if T.rank_of(c) is None and topo.may_write(c, x_dst)]
    same = [c for c in ok if topo.die(c) == topo.die(x_dst)]
    return (same or ok)[0]


def rank_program(g, core, T, topo):
    S = T.sem
    chips, members = _layout(T, topo)
    nch = len(chips)
    roles = [_roles(members[ch], topo) for ch in chips]
    relays = [_relay(roles[i][0], T, topo) for i in range(nch)]

    def cols(c, n=1):
        j = T.rank_of(c)
        return slice(j * B, (j + n) * B)

    def blk(c):
        return T.ag[:, cols(c)]

    def did(c):
        rid, pid, _ = topo.addr(c)
        return DstId(rid=rid, pnc=pid)

    def one(dsts, mask, sem, c):
        return RemoteDMATransfer(dst_ids=[did(d) for d in dsts], dma_engine_mask=mask, remote_sem=sem,
                                 srcs=[blk(c)], dsts=[blk(c) for _ in dsts])

    rank = T.rank_of(core)
    if rank is None:
        if core in relays:
            i = relays.index(core)
            x_src, x_dst = roles[(i - 2) % nch][0], roles[i][0]
            m = topo.mask(core, x_dst)
            g.wait_ge(S.pe, _count(topo.mask(x_src, core)))
            g.remote_dma_fused([one([x_dst], m, S.d2, x_src)], local_sem=S.sent)
            g.wait_ge(S.sent, _count(m))
        return

    ci = chips.index(topo.chip(core))
    mine = members[chips[ci]]
    p = mine.index(core)
    peers = [c for c in mine if c != core]
    X, P = roles[ci]
    xp, pp = mine.index(X), mine.index(P)

    def src_chip(s):
        return members[chips[(ci - s) % nch]]

    def dst_chip(s):
        return members[chips[(ci + s) % nch]]

    on = topo.mask(core, peers[0])
    off = topo.mask(core, dst_chip(1)[0])
    on_only = on & ~off
    halves = _split(off, 2)
    n_pe = len(peers) * _count(on_only)
    n_off, n_half, n_on = _count(off), _count(halves[0]), _count(on)
    n_d = {1: n_off, 2: n_off, 3: n_half if p in (xp, pp) else n_off}

    g.sync.dma_start(blk(core), T.a[:]).then_inc(S.la, 16)
    g.scalar.dma_start(T.wbuf[:], T.w[:]).then_inc(S.lw, 16)

    sent = 0
    g.wait_ge(S.la, 16)
    first = one(peers, on_only, S.pe, core)
    if core == X:
        g.remote_dma_fused([first, one([relays[(ci + 2) % nch]], off, S.pe, core)], local_sem=S.sent)
        g.remote_dma_fused([one([dst_chip(1)[p]], off, S.d1, core)], local_sem=S.sent)
        sent += _count(on_only) + 2 * n_off
    else:
        g.remote_dma_fused([first, one([dst_chip(1)[p]], off, S.d1, core)], local_sem=S.sent)
        g.remote_dma_fused([one([dst_chip(2)[p]], off, S.d2, core)], local_sem=S.sent)
        sent += _count(on_only) + 2 * n_off
        if core == P:
            g.wait_ge(S.pe, n_pe)
            g.remote_dma_fused([one([dst_chip(3)[p]], halves[0], S.d3, core),
                                one([dst_chip(3)[xp]], halves[1], S.d3, X)], local_sem=S.sent)
        else:
            g.remote_dma_fused([one([dst_chip(3)[p]], off, S.d3, core)], local_sem=S.sent)
        sent += n_off
    for s in (1, 2, 3):
        g.wait_ge(S["d%d" % s], n_d[s])
        g.remote_dma_fused([one(peers, on, S["f%d%d" % (s, p)], src_chip(s)[p])], local_sem=S.sent)
        sent += n_on
    g.wait_ge(S.sent, sent)

    others = [q for q in range(len(mine)) if q != p]
    if p == xp:
        seq = [(1, p), (2, p), (3, p)] + [(s, q) for s in (1, 2, 3) for q in others]
    else:
        o = [q for q in others if q != xp][0]
        seq = [(1, p), (2, p), (1, o), (3, p), (1, xp), (2, o), (2, xp), (3, o), (3, xp)]
    bank = {}
    for sq in seq:
        if sq[0] != 1:
            bank[sq] = 2 + len(bank)

    te = g.tensor

    def mm(ps, col, c, sem):
        te.matmul(ps[:, col:col + B], blk(c), T.wbuf[:], True, True).then_inc(sem, 1)

    te.wait_ge(S.la, 16)
    te.wait_ge(S.lw, 16)
    mm(T.ps0, p * B, core, S.mm0)
    te.wait_ge(S.pe, n_pe)
    for c in peers:
        mm(T.ps0, mine.index(c) * B, c, S.mm0)
    for (s, q) in seq:
        if q == p:
            te.wait_ge(S["d%d" % s], n_d[s])
        else:
            te.wait_ge(S["f%d%d" % (s, q)], n_on)
        if s == 1:
            mm(T.ps1, q * B, src_chip(1)[q], S.mm1)
        else:
            mm(T["ps%d" % bank[(s, q)]], 0, src_chip(s)[q], S["mm%d" % bank[(s, q)]])

    ve = g.vector
    ng = len(mine)

    def group(s):
        return cols(src_chip(s)[0], ng)

    ve.wait_ge(S.mm0, ng)
    ve.tensor_copy(T.out[:, group(0)], T.ps0[:, 0:ng * B]).then_inc(S.cp0, 1)
    seen = 0
    for (s, q) in seq:
        if s == 1:
            seen += 1
            if seen == ng:
                ve.wait_ge(S.mm1, ng)
                ve.tensor_copy(T.out[:, group(1)], T.ps1[:, 0:ng * B]).then_inc(S.cp1, 1)
        else:
            k = bank[(s, q)]
            ve.wait_ge(S["mm%d" % k], 1)
            ve.tensor_copy(T.out[:, cols(src_chip(s)[q])], T["ps%d" % k][:, 0:B]).then_inc(
                S.cp2 if s == 2 else S["cp3%d" % q], 1)

    last = [q for (s, q) in seq if s == 3]
    issued = {"sta": 0, "stb": 0}

    def store(queue, name, sem, need, cs):
        queue.wait_ge(sem, need)
        queue.dma_start(T.y[:, cs], T.out[:, cs]).then_inc(S[name], 16)
        issued[name] += 16

    store(g.sync, "sta", S.cp0, 1, group(0))
    store(g.scalar, "stb", S["cp3%d" % last[0]], 1, cols(src_chip(3)[last[0]]))
    store(g.scalar, "stb", S.cp1, 1, group(1))
    store(g.sync, "sta", S.cp2, ng, group(2))
    store(g.scalar, "stb", S["cp3%d" % last[1]], 1, cols(src_chip(3)[last[1]]))
    store(g.sync, "sta", S["cp3%d" % last[2]], 1, cols(src_chip(3)[last[2]]))
    g.sync.wait_ge(S.sta, issued["sta"])
    g.scalar.wait_ge(S.stb, issued["stb"])
